import numpy as np
import ml_dtypes

BF16 = ml_dtypes.bfloat16


def bf(x):
    return np.asarray(x, np.float32).astype(BF16)


def f32(x):
    return np.asarray(x, np.float32)


def f64(x):
    return np.asarray(x).astype(np.float64)


def striped(idx):
    return np.tile(idx.reshape(-1, 16).T, (8, 1))


S, K, M, N, D = 256, 256, 128, 128, 256


def setup_inputs():
    return {"table": bf(np.random.standard_normal((K, S))), "qw": bf(np.random.standard_normal((K, M)) / np.sqrt(K)), "kw": bf(np.random.standard_normal((K, M)) / np.sqrt(K)), "w": bf(np.random.standard_normal((K, D)) / np.sqrt(K)), "offs": striped(np.sort(np.random.permutation(S)[:N]))}


def reference(table, qw, kw, w, offs):
    idx = offs[:16].T.reshape(-1)
    x = f64(table)[:, idx]
    a = (f64(qw).T @ x).T @ (f64(kw).T @ x) / np.sqrt(M)
    a = np.exp(a - a.max(axis=1, keepdims=True))
    a = a / a.sum(axis=1, keepdims=True)
    return a @ (f64(w).T @ x).T

@@ -1,0 +1,81 @@
+import math
+
+import concourse.mybir as mybir
+from concourse.masks import make_identity
+
+BF16, F32, U16 = mybir.dt.bfloat16, mybir.dt.float32, mybir.dt.uint16
+ACT, ALU, AXIS = mybir.ActivationFunctionType, mybir.AluOpType, mybir.AxisListType
+
+P = 128
+S, K, M, N, D = 256, 256, 128, 128, 256
+FLOPS = 2 * K * N * (2 * M + D) + 2 * M * N * N + 2 * N * N * D
+
+
+def tile_rows_pruneattn_srt_kernel(tc, table, qw, kw, w, offs, out):
+    nc = tc.nc
+    k_blocks, d_blocks = K // P, D // P
+    with (
+        tc.tile_pool(name="sbuf", bufs=1) as sbuf,
+        tc.psum_pool(name="psum", bufs=1) as psum,
+    ):
+        tokens = sbuf.tile([P, k_blocks, S], BF16)
+        offsets = sbuf.tile([P, N // 16], U16)
+        q_weights = sbuf.tile([P, k_blocks, M], BF16)
+        h_weights = sbuf.tile([P, k_blocks, M], BF16)
+        v_weights = sbuf.tile([P, k_blocks, D], BF16)
+        nc.sync.dma_start(tokens[:], table.rearrange("(p a) s -> p a s", a=k_blocks))
+        nc.scalar.dma_start(q_weights[:], qw.rearrange("(p a) m -> p a m", a=k_blocks))
+        nc.sync.dma_start(offsets[:], offs)
+        nc.scalar.dma_start(h_weights[:], kw.rearrange("(p a) m -> p a m", a=k_blocks))
+        nc.sync.dma_start(v_weights[:], w.rearrange("(p a) d -> p a d", a=k_blocks))
+
+        identity = sbuf.tile([P, P], BF16)
+        make_identity(nc, identity[:])
+
+        def project(bank, weights, first):
+            for a in range(k_blocks):
+                nc.tensor.matmul(bank, weights[:, a, first : first + P], tokens[:, a, :].indirect(offsets[:]),
+                                 start=(a == 0), stop=(a == k_blocks - 1))
+
+        q_bank = psum.tile([P, N], F32)
+        h_bank = psum.tile([P, N], F32)
+        project(q_bank[:], q_weights, 0)
+        project(h_bank[:], h_weights, 0)
+        q = sbuf.tile([P, N], BF16)
+        h = sbuf.tile([P, N], BF16)
+        nc.vector.tensor_scalar(q[:], q_bank[:], 1.0 / math.sqrt(M), None, ALU.mult)
+        nc.scalar.copy(h[:], h_bank[:])
+
+        v_bank = psum.tile([P, d_blocks, N], F32)
+        for b in range(d_blocks):
+            project(v_bank[:, b, :], v_weights, b * P)
+
+        scores = psum.tile([P, N], F32)
+        nc.tensor.matmul(scores[:], q[:], h[:], start=True, stop=True)
+        neg_max = sbuf.tile([P, 1], F32)
+        nc.vector.tensor_reduce(neg_max[:], scores[:], AXIS.X, ALU.max, negate=True)
+
+        v = sbuf.tile([P, d_blocks, N], BF16)
+        nc.scalar.copy(v[:], v_bank[:])
+        v_flipped_bank = psum.tile([P, D], BF16)
+        for b in range(d_blocks):
+            nc.tensor.transpose(v_flipped_bank[:, b * P : (b + 1) * P], v[:, b, :], identity[:])
+        v_flipped = sbuf.tile([P, D], BF16)
+        nc.vector.tensor_copy(v_flipped[:], v_flipped_bank[:])
+
+        e = sbuf.tile([P, N], BF16)
+        row_sum = sbuf.tile([P, 1], F32)
+        nc.scalar.activation(e[:], scores[:], ACT.Exp, bias=neg_max[:], accum_out=row_sum[:])
+        inv_sum = sbuf.tile([P, 1], F32)
+        nc.vector.reciprocal(inv_sum[:], row_sum[:])
+
+        e_flipped_bank = psum.tile([P, N], BF16)
+        nc.tensor.transpose(e_flipped_bank[:], e[:], identity[:])
+        e_flipped = sbuf.tile([P, N], BF16)
+        nc.vector.tensor_copy(e_flipped[:], e_flipped_bank[:])
+
+        out_bank = psum.tile([P, D], F32)
+        nc.tensor.matmul(out_bank[:], e_flipped[:], v_flipped[:], start=True, stop=True)
+        result = sbuf.tile([P, D], F32)
+        nc.vector.tensor_scalar(result[:], out_bank[:], inv_sum[:], None, ALU.mult)
+        nc.sync.dma_start(out, result[:])

@@ -8,6 +8,7 @@ ACT, ALU, AXIS = mybir.ActivationFunctionType, mybir.AluOpType, mybir.AxisListTy
 
 P = 128
 S, K, M, N, D = 256, 256, 128, 128, 256
+WARM_UP_MATMULS = 12
 FLOPS = 2 * K * N * (2 * M + D) + 2 * M * N * N + 2 * N * N * D
 
 
@@ -28,6 +29,12 @@ def tile_rows_pruneattn_srt_kernel(tc, table, qw, kw, w, offs, out):
         nc.sync.dma_start(offsets[:], offs)
         nc.scalar.dma_start(h_weights[:], kw.rearrange("(p a) m -> p a m", a=k_blocks))
         nc.sync.dma_start(v_weights[:], w.rearrange("(p a) d -> p a d", a=k_blocks))
+
+        zeros = sbuf.tile([P, P], BF16)
+        nc.vector.memset(zeros[:], 0.0)
+        warm_bank = psum.tile([P, P], F32)
+        for step in range(WARM_UP_MATMULS):
+            nc.tensor.matmul(warm_bank[:], zeros[:], zeros[:], start=True, stop=True)
 
         identity = sbuf.tile([P, P], BF16)
         make_identity(nc, identity[:])

import math

import concourse.mybir as mybir
from concourse.masks import make_identity

BF16, F32, U16 = mybir.dt.bfloat16, mybir.dt.float32, mybir.dt.uint16
ACT, ALU, AXIS = mybir.ActivationFunctionType, mybir.AluOpType, mybir.AxisListType

P = 128
S, K, M, N, D = 256, 256, 128, 128, 256
WARM_UP_MATMULS = 12
FLOPS = 2 * K * N * (2 * M + D) + 2 * M * N * N + 2 * N * N * D


def tile_rows_pruneattn_srt_kernel(tc, table, qw, kw, w, offs, out):
    nc = tc.nc
    k_blocks, d_blocks = K // P, D // P
    with (
        tc.tile_pool(name="sbuf", bufs=1) as sbuf,
        tc.psum_pool(name="psum", bufs=1) as psum,
    ):
        tokens = sbuf.tile([P, k_blocks, S], BF16)
        offsets = sbuf.tile([P, N // 16], U16)
        q_weights = sbuf.tile([P, k_blocks, M], BF16)
        h_weights = sbuf.tile([P, k_blocks, M], BF16)
        v_weights = sbuf.tile([P, k_blocks, D], BF16)
        nc.sync.dma_start(tokens[:], table.rearrange("(p a) s -> p a s", a=k_blocks))
        nc.scalar.dma_start(q_weights[:], qw.rearrange("(p a) m -> p a m", a=k_blocks))
        nc.sync.dma_start(offsets[:], offs)
        nc.scalar.dma_start(h_weights[:], kw.rearrange("(p a) m -> p a m", a=k_blocks))
        nc.sync.dma_start(v_weights[:], w.rearrange("(p a) d -> p a d", a=k_blocks))

        zeros = sbuf.tile([P, P], BF16)
        nc.vector.memset(zeros[:], 0.0)
        warm_bank = psum.tile([P, P], F32)
        for step in range(WARM_UP_MATMULS):
            nc.tensor.matmul(warm_bank[:], zeros[:], zeros[:], start=True, stop=True)

        identity = sbuf.tile([P, P], BF16)
        make_identity(nc, identity[:])

        def project(bank, weights, first):
            for a in range(k_blocks):
                nc.tensor.matmul(bank, weights[:, a, first : first + P], tokens[:, a, :].indirect(offsets[:]),
                                 start=(a == 0), stop=(a == k_blocks - 1))

        q_bank = psum.tile([P, N], F32)
        h_bank = psum.tile([P, N], F32)
        project(q_bank[:], q_weights, 0)
        project(h_bank[:], h_weights, 0)
        q = sbuf.tile([P, N], BF16)
        h = sbuf.tile([P, N], BF16)
        nc.vector.tensor_scalar(q[:], q_bank[:], 1.0 / math.sqrt(M), None, ALU.mult)
        nc.scalar.copy(h[:], h_bank[:])

        v_bank = psum.tile([P, d_blocks, N], F32)
        for b in range(d_blocks):
            project(v_bank[:, b, :], v_weights, b * P)

        scores = psum.tile([P, N], F32)
        nc.tensor.matmul(scores[:], q[:], h[:], start=True, stop=True)
        neg_max = sbuf.tile([P, 1], F32)
        nc.vector.tensor_reduce(neg_max[:], scores[:], AXIS.X, ALU.max, negate=True)

        v = sbuf.tile([P, d_blocks, N], BF16)
        nc.scalar.copy(v[:], v_bank[:])
        v_flipped_bank = psum.tile([P, D], BF16)
        for b in range(d_blocks):
            nc.tensor.transpose(v_flipped_bank[:, b * P : (b + 1) * P], v[:, b, :], identity[:])
        v_flipped = sbuf.tile([P, D], BF16)
        nc.vector.tensor_copy(v_flipped[:], v_flipped_bank[:])

        e = sbuf.tile([P, N], BF16)
        row_sum = sbuf.tile([P, 1], F32)
        nc.scalar.activation(e[:], scores[:], ACT.Exp, bias=neg_max[:], accum_out=row_sum[:])
        inv_sum = sbuf.tile([P, 1], F32)
        nc.vector.reciprocal(inv_sum[:], row_sum[:])

        e_flipped_bank = psum.tile([P, N], BF16)
        nc.tensor.transpose(e_flipped_bank[:], e[:], identity[:])
        e_flipped = sbuf.tile([P, N], BF16)
        nc.vector.tensor_copy(e_flipped[:], e_flipped_bank[:])

        out_bank = psum.tile([P, D], F32)
        nc.tensor.matmul(out_bank[:], e_flipped[:], v_flipped[:], start=True, stop=True)
        result = sbuf.tile([P, D], F32)
        nc.vector.tensor_scalar(result[:], out_bank[:], inv_sum[:], None, ALU.mult)
        nc.sync.dma_start(out, result[:])
